import numpy as np
import ml_dtypes


def mxq(x, axis, fmt="e4m3"):
    dtype, down = {"e4m3": (ml_dtypes.float8_e4m3fn, 7), "e5m2": (ml_dtypes.float8_e5m2, 14)}[fmt]
    v = np.moveaxis(np.asarray(x, np.float32).astype(ml_dtypes.bfloat16).astype(np.float64), axis, -1)
    blocks = v.reshape(v.shape[:-1] + (-1, 32))
    amax = np.abs(blocks).max(-1, keepdims=True)
    byte = np.maximum(np.where(amax > 0, np.frexp(amax)[1] - 1 + 127, 0) - down, 1)
    scale = np.exp2(byte - 127.0)
    codes = (blocks / scale).astype(np.float32).astype(dtype).astype(np.float64)
    return np.moveaxis((codes * scale).reshape(v.shape), -1, axis)


WIDE = False


def mx_kscale(k):
    if not WIDE:
        return np.ones(k)
    levels = np.array([10, -10, 5, -5, 0])
    if k % 512:
        return np.exp2(np.random.permutation(np.resize(levels, k // 32))).repeat(32)
    a = np.empty((k // 512, 16))
    for p in range(k // 512):
        a[p, :8] = np.random.permutation(np.resize(levels, 8))
        for g in range(8):
            far = levels[np.abs(levels - a[p, g]) >= 10]
            a[p, g + 8] = far[np.random.randint(len(far))]
    return np.exp2(a.ravel()).repeat(32)


def f64(x):
    return np.asarray(x).astype(np.float64)


def striped(idx):
    return np.tile(idx.reshape(-1, 16).T, (8, 1)).astype(np.uint16)


def unstriped(offs):
    return offs[:16].T.reshape(-1).astype(np.int64)


def striped8(idx):
    return np.concatenate([x.reshape(-1, 16).T for x in idx]).astype(np.uint16)


def runs(offs, k):
    lists = np.stack([offs[16 * r : 16 * r + 16].T.reshape(-1) for r in range(8)]).astype(np.int64)
    return lists[np.arange(k) % 512 // 64]


def pack_weight(w):
    k, n = w.shape
    w = f64(np.asarray(w, np.float32).astype(ml_dtypes.bfloat16)).reshape(k // 32, 32, n)
    amax = np.abs(w).max(1)
    byte = np.clip(np.where(amax > 0, np.frexp(amax)[1] - 1 + 127 - 7, 1), 1, 254)
    scaled = (w * np.exp2(127.0 - byte)[:, None, :]).reshape(k, n).astype(np.float32)
    words = np.ascontiguousarray(scaled.reshape(k // 512, 128, 4, n).transpose(0, 1, 3, 2)).astype(ml_dtypes.float8_e4m3fn).view(np.uint8)
    return words, np.ascontiguousarray(byte.astype(np.uint8).reshape(k // 512, 16, n))


def unpack_weight(words, scales):
    g, p, n, _ = words.shape
    vals = np.ascontiguousarray(words).view(ml_dtypes.float8_e4m3fn).astype(np.float64) * np.repeat(np.exp2(scales.astype(np.float64) - 127.0), 8, axis=1)[..., None]
    return vals.transpose(0, 1, 3, 2).reshape(g * 512, n)

def planes(y):
    n, m = y.shape
    v = y.astype(np.float32).astype(ml_dtypes.bfloat16).astype(np.float64).reshape(n // 32, 32, m)
    top = np.abs(v).max(1)
    byte = np.clip(np.where(top > 0, np.frexp(top)[1] - 1 + 127 - 7, 1), 1, 254)
    codes = (v * np.exp2(127.0 - byte)[:, None, :]).reshape(n, m).astype(np.float32).astype(ml_dtypes.float8_e4m3fn).view(np.uint8)
    words = codes.reshape(n // 512, 128, 4, m).transpose(0, 1, 3, 2)
    return np.ascontiguousarray(words), np.ascontiguousarray(byte.astype(np.uint8).reshape(n // 512, 16, m))


K, T, S, N, G, H, W, U = 512, 1024, 256, 512, 2048, 512, 128, 1024


def setup_inputs():
    n = np.random.standard_normal
    s = mx_kscale(K)[:, None]
    u = mx_kscale(K)
    packed_xT = pack_weight(n((K, T)) * s)
    packed_dT = pack_weight(n((K, G)) / s)
    packed_w1 = pack_weight(n((H, N)) / np.sqrt(2 * H) / u[:, None])
    packed_w2 = pack_weight(n((H, N)) / np.sqrt(2 * H) / u[:, None])
    perm = np.random.permutation(S)
    return {
        "x_words": packed_xT[0],
        "x_scales": packed_xT[1],
        "d_words": packed_dT[0],
        "d_scales": packed_dT[1],
        "gn": (np.random.uniform(0.5, 1.5, (H, 1)) * u[:, None]).astype(np.float32),
        "gm": (np.random.uniform(0.5, 1.5, (H, 1)) * u[:, None]).astype(np.float32),
        "w1_words": packed_w1[0],
        "w1_scales": packed_w1[1],
        "w2_words": packed_w2[0],
        "w2_scales": packed_w2[1],
        "offs": striped(np.random.permutation(T)[:S]),
        "k1": striped8(np.random.randint(0, G, (8, H))),
        "two": striped(np.random.permutation(T)[:S]),
        "k2": striped8(np.random.randint(0, G, (8, H))),
        "n1": striped(perm[:W]),
        "n2": striped(perm[W:]),
        "n3": striped8(np.stack([np.random.permutation(S) for _ in range(8)])),
        "n4": striped8(np.stack([np.random.permutation(S) for _ in range(8)])),
        "n5": striped(np.random.randint(0, S, U)),
    }


def reference(x_words, x_scales, d_words, d_scales, gn, gm, w1_words, w1_scales, w2_words, w2_scales, offs, k1, two, k2, n1, n2, n3, n4, n5):
    d_k1 = unpack_weight(d_words, d_scales)[np.arange(K)[:, None], runs(k1, K)]
    xq = unpack_weight(x_words, x_scales)[:, unstriped(offs)]
    a = 0.0625 * (d_k1.T @ xq)
    pa = a[:, unstriped(n1)]
    pb = a[:, unstriped(n2)]
    rb = np.maximum(pa, pb)
    ra = pa / (np.abs(pb) + 0.5)
    ds = np.zeros((H, S))
    ds[:, unstriped(n1)] = ra
    dt = ds.copy()
    dt[:, unstriped(n2)] = rb
    z = f64(gn) * dt
    d_k2 = unpack_weight(d_words, d_scales)[np.arange(K)[:, None], runs(k2, K)]
    x_two = unpack_weight(x_words, x_scales)[:, unstriped(two)]
    b = 0.0625 * (d_k2.T @ x_two)
    pa2 = b[np.arange(H)[:, None], runs(n3, H)]
    pb2 = b[np.arange(H)[:, None], runs(n4, H)]
    mu = 0.3125 * (b + pa2 + pb2)
    z2 = f64(gm) * ((b - mu) / (np.sqrt((pa2 - mu) ** 2 + (pb2 - mu) ** 2 + 0.25)))
    h = unpack_weight(w1_words, w1_scales).T @ mxq(z, 0, "e4m3") + unpack_weight(w2_words, w2_scales).T @ mxq(z2, 0, "e4m3")
    mb = h[:, unstriped(n5)]
    mx = mb.reshape(N, S, 4).max(axis=2)
    out_0 = h - mx
    return (out_0,) + planes(out_0)

@@ -1,0 +1,308 @@
+from contextlib import ExitStack
+
+import concourse.mybir as mybir
+
+K, T, S, N, G, H, W, U = 512, 1024, 256, 512, 2048, 512, 128, 1024
+FLOPS = 2 * 2 * K * H * S + 2 * 2 * H * N * S
+
+F32 = mybir.dt.float32
+BF16 = mybir.dt.bfloat16
+I32 = mybir.dt.int32
+U32 = mybir.dt.uint32
+U16 = mybir.dt.uint16
+U8 = mybir.dt.uint8
+FP8X4 = mybir.dt.float8_e4m3fn_x4
+ALU = mybir.AluOpType
+ACT = mybir.ActivationFunctionType
+AXIS = mybir.AxisListType
+
+P = 128
+PACK = 4
+CHUNK = 64
+MEMBERS = 4
+
+
+def words_of(dram):
+    return dram[0].rearrange("p n t -> p (n t)").bitcast(I32)
+
+
+def deal(engine, out, in_, run):
+    engine.tensor_copy(
+        out=out.rearrange("p (t c i) -> p c t i", t=PACK, i=run),
+        in_=in_.rearrange("p (c i t) -> p c t i", t=PACK, i=run),
+    )
+
+
+def interleave(nc, out, in_):
+    nc.vector.tensor_copy(
+        out=out.rearrange("p (c i) t -> p c t i", i=4),
+        in_=in_.rearrange("p t (c i) -> p c t i", i=4),
+    )
+
+
+def tile_picked_pqjratiostdgmaxd_none_po_kernel(
+    tc, x_words, x_scales, d_words, d_scales, gn, gm, w1_words, w1_scales, w2_words, w2_scales,
+    offs, k1, two, k2, n1, n2, n3, n4, n5, out_0, out_1, out_2,
+):
+    nc = tc.nc
+    with ExitStack() as ctx:
+        held = ctx.enter_context(tc.tile_pool(name="held", bufs=1))
+        sb = ctx.enter_context(tc.tile_pool(name="sb", bufs=1))
+        psum = ctx.enter_context(tc.psum_pool(name="psum", bufs=1))
+
+        def tile(name, shape, dtype, tag=None):
+            return sb.tile(shape, dtype, name=name, tag=tag or name, align_bytes=64)
+
+        def load_list(name, dram):
+            offsets = held.tile(list(dram.shape), U16, name=name)
+            nc.sync.dma_start(offsets[:], dram)
+            return offsets
+
+        d_bytes = tile("d_bytes", [P, G], U8)
+        x_bytes = tile("x_bytes", [P, T], U8)
+        nc.vector.memset(d_bytes[:].bitcast(I32), 0)
+        nc.vector.memset(x_bytes[:].bitcast(I32), 0)
+        nc.scalar.dma_start(d_bytes[0:P:8, :].bitcast(I32), d_scales[0].bitcast(I32))
+        nc.scalar.dma_start(x_bytes[0:P:8, :].bitcast(I32), x_scales[0].bitcast(I32))
+        k2_l = load_list("k2_l", k2)
+        two_l = load_list("two_l", two)
+        k1_l = load_list("k1_l", k1)
+        offs_l = load_list("offs_l", offs)
+        n3_l = load_list("n3_l", n3)
+        x_table = tile("x_table", [P, T], U32)
+        d_table = tile("d_table", [P, G], U32)
+        nc.sync.dma_start(d_table[:].bitcast(I32), words_of(d_words))
+        nc.sync.dma_start(x_table[:].bitcast(I32), words_of(x_words))
+        n4_l = load_list("n4_l", n4)
+        n2_l = load_list("n2_l", n2)
+        n1_l = load_list("n1_l", n1)
+        n5_l = load_list("n5_l", n5)
+
+        planes = [tile(f"plane{i}", [P, H + S], U8) for i in range(2)]
+        for plane in planes:
+            nc.vector.memset(plane[:].bitcast(I32), 0)
+        quarter = tile("quarter", [P, 1], F32)
+        nc.vector.memset(quarter[:], 0.25)
+        half_bias = tile("half_bias", [P, 1], F32)
+        nc.vector.memset(half_bias[:], 0.5)
+        rows = [tile(f"rows{t}", [P, 2 * S], F32) for t in range(PACK)]
+        for t in range(PACK):
+            nc.vector.memset(rows[t][:, S : 2 * S], 0.0)
+
+        def coded_layer(name, codes_l, tokens_l, plane, queue, slots):
+            picked_db = tile(f"{name}_db", [P, H], U8, slots[0])
+            picked_xb = tile(f"{name}_xb", [P, S], U8, slots[1])
+            staged = tile(f"{name}_staged", [P, H + S], U8)
+            nc.vector.tensor_copy(picked_db[:], d_bytes[:].indirect(codes_l[:]))
+            nc.vector.tensor_copy(picked_xb[:], x_bytes[:].indirect(tokens_l[:]))
+            deal(nc.vector, staged[:, 0:H], picked_db[:], 16)
+            nc.vector.tensor_copy(staged[:, H : H + S].bitcast(I32), picked_xb[:].bitcast(I32))
+            for q in range(4):
+                queue.dma_start(
+                    plane[32 * q : 32 * q + 4, :].bitcast(I32),
+                    staged[32 * q : 32 * q + 32 : 8, :].bitcast(I32),
+                )
+            picked_dw = tile(f"{name}_dw", [P, H], U32, slots[2])
+            picked_xw = tile(f"{name}_xw", [P, S], U32, slots[3])
+            dealt_dw = tile(f"{name}_dealt", [P, H], U32)
+            nc.vector.tensor_copy(picked_dw[:], d_table[:].indirect(codes_l[:]))
+            nc.vector.tensor_copy(picked_xw[:], x_table[:].indirect(tokens_l[:]))
+            deal(nc.vector, dealt_dw[:], picked_dw[:], 4)
+            banks = []
+            for t in range(PACK):
+                bank = psum.tile([P, S], F32, name=f"{name}_bank{t}", tag=f"{name}_bank{t}")
+                cols = slice(P * t, P * (t + 1))
+                nc.tensor.matmul_mx(
+                    out=bank[:],
+                    lhsT=dealt_dw[:, cols].bitcast(FP8X4),
+                    lhsT_scale=plane[:, cols],
+                    rhs=picked_xw[:].bitcast(FP8X4),
+                    rhs_scale=plane[:, H : H + S],
+                    start=True,
+                    stop=True,
+                )
+                banks.append(bank)
+            return banks
+
+        b_banks = coded_layer("b", k2_l, two_l, planes[0], nc.scalar, ("relay", "b_x", "relay", "b_x"))
+        gains = tile("gains", [P, 2, 8], F32, "plane0")
+        gn_t = gains[:, 0, 0:PACK]
+        gm_t = gains[:, 1, 0:PACK]
+        nc.sync.dma_start(gn_t, gn.rearrange("(p t) o -> p (t o)", t=PACK))
+        nc.sync.dma_start(gm_t, gm.rearrange("(p t) o -> p (t o)", t=PACK))
+        a_banks = coded_layer("a", k1_l, offs_l, planes[1], nc.sync, ("relay", "b_staged", "b_staged", "relay"))
+
+        w_raw = tile("w_raw", [P, 2, N], U32, "a_staged")
+        nc.sync.dma_start(w_raw[:, 0, :].bitcast(I32), words_of(w1_words))
+        nc.sync.dma_start(w_raw[:, 1, :].bitcast(I32), words_of(w2_words))
+        w_bytes_raw = tile("w_bytes_raw", [P, N], U8, "plane1")
+        nc.vector.memset(w_bytes_raw[:].bitcast(I32), 0)
+        for i, scales in enumerate((w1_scales, w2_scales)):
+            for q in range(4):
+                nc.sync.dma_start(
+                    w_bytes_raw[32 * q + 4 * i : 32 * q + 4 * i + 4, :].bitcast(I32),
+                    scales[0][4 * q : 4 * q + 4, :].bitcast(I32),
+                )
+
+        pairs = ((0, 1), (2, 3))
+        fetched = [tile(f"fetched{h}", [P, 2, 2, S], F32) for h in range(2)]
+        for h in range(2):
+            for t in pairs[h]:
+                nc.scalar.activation(rows[t][:, 0:S], b_banks[t][:], ACT.Copy, scale=0.0625)
+            for t in pairs[h]:
+                nc.scalar.activation(fetched[h][:, 0, t % 2, :], rows[t][:].indirect(n3_l[:]), ACT.Copy)
+                nc.scalar.activation(fetched[h][:, 1, t % 2, :], rows[t][:].indirect(n4_l[:]), ACT.Copy)
+
+        pa = [tile(f"pa{h}", [P, 2, W], F32) for h in range(2)]
+        pb = [tile(f"pb{h}", [P, 2, W], F32) for h in range(2)]
+        size = [tile(f"size{h}", [P, 2, W], F32) for h in range(2)]
+        den2 = [tile(f"den2_{h}", [P, 2, W], F32) for h in range(2)]
+        inv = [tile(f"inv{h}", [P, 2, W], F32) for h in range(2)]
+        for h in range(2):
+            for t in pairs[h]:
+                a_t = rows[t][:, S : 2 * S]
+                nc.scalar.activation(a_t, a_banks[t][:], ACT.Copy, scale=0.0625)
+                nc.scalar.activation(pb[h][:, t % 2, :], a_t.indirect(n2_l[:]), ACT.Copy)
+                nc.scalar.activation(pa[h][:, t % 2, :], a_t.indirect(n1_l[:]), ACT.Copy)
+            nc.scalar.activation(size[h][:], pb[h][:], ACT.Abs)
+            nc.scalar.activation(den2[h][:], size[h][:], ACT.Square, bias=half_bias[:])
+            nc.scalar.activation(inv[h][:], den2[h][:], ACT.Abs_reciprocal_sqrt)
+
+        sq = [tile(f"sq{h}", [P, 2, 2, S], F32) for h in range(2)]
+        centred = [tile(f"centred{h}", [P, 2, S], F32) for h in range(2)]
+        spread = [tile(f"spread{h}", [P, 2, S], F32) for h in range(2)]
+        inv2 = [tile(f"inv2_{h}", [P, 2, S], F32) for h in range(2)]
+        terms, ra, rb, dt = {}, {}, {}, {}
+
+        def b_sums(h, slot):
+            terms[h] = tile(f"terms{h}", [P, 3, 2, S], F32, slot)
+            nc.vector.tensor_tensor(terms[h][:, 2], fetched[h][:, 0], fetched[h][:, 1], ALU.add)
+            nc.vector.tensor_tensor(terms[h][:, 1], fetched[h][:, 0], fetched[h][:, 1], ALU.subtract)
+
+        def b_spread(h):
+            for t in pairs[h]:
+                nc.vector.scalar_tensor_tensor(
+                    terms[h][:, 0, t % 2, :], terms[h][:, 2, t % 2, :], -0.6, rows[t][:, 0:S], ALU.mult, ALU.add
+                )
+            for t in pairs[h]:
+                nc.vector.scalar_tensor_tensor(
+                    centred[h][:, t % 2, :], terms[h][:, 2, t % 2, :], -5.0 / 11.0, rows[t][:, 0:S], ALU.mult, ALU.add
+                )
+            nc.vector.tensor_tensor(sq[h][:], terms[h][:, 0:2], terms[h][:, 0:2], ALU.mult)
+            nc.vector.scalar_tensor_tensor(spread[h][:], sq[h][:, 0], 0.390625, sq[h][:, 1], ALU.mult, ALU.add)
+            nc.scalar.activation(inv2[h][:], spread[h][:], ACT.Abs_reciprocal_sqrt, bias=quarter[:], scale=0.5)
+
+        def b_finish(h):
+            for t in pairs[h]:
+                nc.vector.scalar_tensor_tensor(
+                    z2_rows[:, t, :], centred[h][:, t % 2, :], gm_s[:, t : t + 1], inv2[h][:, t % 2, :],
+                    ALU.mult, ALU.mult,
+                )
+
+        def larger(h, slot):
+            rb[h] = tile(f"rb{h}", [P, 2, W], F32, slot)
+            nc.vector.tensor_tensor(rb[h][:], pa[h][:], pb[h][:], ALU.max)
+
+        def ratio(h, slot):
+            ra[h] = tile(f"ra{h}", [P, 2, W], F32, slot)
+            nc.vector.tensor_tensor(ra[h][:], pa[h][:], inv[h][:], ALU.mult)
+
+        def scatters(h):
+            for t in pairs[h]:
+                dt[t] = tile(f"dt{t}", [P, S], F32)
+                nc.scalar.activation(dt[t][:].indirect(n2_l[:]), rb[h][:, t % 2, :], ACT.Copy)
+            for t in pairs[h]:
+                nc.scalar.activation(dt[t][:].indirect(n1_l[:]), ra[h][:, t % 2, :], ACT.Copy)
+
+        def z_round(t):
+            nc.vector.tensor_scalar(z_bf[:, :, t], dt[t][:], gn_t[:, t : t + 1], None, ALU.mult)
+
+        b_sums(0, "b_staged")
+        b_spread(0)
+        larger(0, "b_staged")
+        b_sums(1, "terms1")
+        ratio(0, "fetched1")
+        scatters(0)
+        b_spread(1)
+        larger(1, "terms1")
+        ratio(1, "sq0")
+        scatters(1)
+
+        w_dealt = [tile(f"w_dealt{i}", [P, N], U32) for i in range(2)]
+        w_plane = tile("w_plane", [P, N], U8)
+        for i in range(2):
+            deal(nc.vector, w_dealt[i][:], w_raw[:, i, :], 4)
+        deal(nc.vector, w_plane[:], w_bytes_raw[:], 16)
+        gm_s = tile("gm_s", [P, PACK], F32)
+        nc.vector.tensor_scalar(gm_s[:], gm_t, 0.6875, None, ALU.mult)
+
+        z2_rows = tile("z2_rows", [P, PACK, S], BF16)
+        z_bf = tile("z_bf", [P, S, PACK], BF16, "sq1")
+        b_finish(0)
+        z_round(0)
+        z_round(1)
+        b_finish(1)
+        z2_bf = tile("z2_bf", [P, S, PACK], BF16)
+        interleave(nc, z2_bf[:], z2_rows[:])
+        z_codes = [tile(f"z_codes{i}", [P, S], U32) for i in range(2)]
+        z_plane = [tile(f"z_plane{i}", [P, S], U8) for i in range(2)]
+        nc.vector.quantize_mx(
+            out=z_codes[1][:].bitcast(FP8X4), scales=z_plane[1][:], in_=z2_bf[:].rearrange("p j t -> p (j t)")
+        )
+        z_round(2)
+        z_round(3)
+        nc.vector.quantize_mx(
+            out=z_codes[0][:].bitcast(FP8X4), scales=z_plane[0][:], in_=z_bf[:].rearrange("p j t -> p (j t)")
+        )
+
+        h_banks = [psum.tile([P, S], F32, name=f"h_bank{t}", tag=f"b_bank{t}") for t in range(PACK)]
+        for i in (1, 0):
+            for t in range(PACK):
+                cols = slice(P * t, P * (t + 1))
+                nc.tensor.matmul_mx(
+                    out=h_banks[t][:],
+                    lhsT=w_dealt[i][:, cols].bitcast(FP8X4),
+                    lhsT_scale=w_plane[4 * i : P, cols],
+                    rhs=z_codes[i][:].bitcast(FP8X4),
+                    rhs_scale=z_plane[i][:],
+                    start=(i == 1),
+                    stop=(i == 0),
+                )
+        for t in range(PACK):
+            nc.vector.tensor_copy(rows[t][:, 0:S], h_banks[t][:])
+
+        out_rows = out_0.rearrange("(p t) j -> p t j", t=PACK)
+        out_words = words_of(out_1)
+        y_codes = tile("y_codes", [P, S], U32)
+        y_plane = tile("y_plane", [P, S], U8)
+        chunks = S // CHUNK
+        for c in range(chunks):
+            cols = slice(CHUNK * c, CHUNK * (c + 1))
+            entries = n5_l[:, CHUNK * MEMBERS // 16 * c : CHUNK * MEMBERS // 16 * (c + 1)]
+            mb = tile(f"mb{c}", [P, PACK, CHUNK, MEMBERS], F32)
+            mx = tile(f"mx{c}", [P, PACK, CHUNK], F32)
+            y = tile(f"y{c}", [P, PACK, CHUNK], F32)
+            y_bf = tile(f"y_bf{c}", [P, CHUNK, PACK], BF16)
+            for t in range(PACK):
+                nc.scalar.activation(mb[:, t].rearrange("p j m -> p (j m)"), rows[t][:].indirect(entries), ACT.Copy)
+            if c < chunks - 1:
+                half = tile(f"half{c}", [P, PACK * CHUNK, 2], F32)
+                flat = mb[:].rearrange("p t j m -> p (t j) m")
+                nc.vector.tensor_tensor(half[:], flat[:, :, 0:2], flat[:, :, 2:4], ALU.max)
+                nc.vector.tensor_tensor(mx[:].rearrange("p t j -> p (t j)"), half[:, :, 0], half[:, :, 1], ALU.max)
+                for t in range(PACK):
+                    nc.vector.tensor_tensor(y[:, t, :], rows[t][:, cols], mx[:, t, :], ALU.subtract)
+                interleave(nc, y_bf[:], y[:])
+            else:
+                for t in range(PACK):
+                    nc.vector.tensor_reduce(mx[:, t, :], mb[:, t], AXIS.X, ALU.max)
+                    nc.vector.tensor_tensor(y_bf[:, :, t], rows[t][:, cols], mx[:, t, :], ALU.subtract)
+                    nc.vector.tensor_tensor(y[:, t, :], rows[t][:, cols], mx[:, t, :], ALU.subtract)
+            nc.sync.dma_start(out_rows[:, :, cols], y[:])
+            nc.vector.quantize_mx(
+                out=y_codes[:, cols].bitcast(FP8X4), scales=y_plane[:, cols], in_=y_bf[:].rearrange("p j t -> p (j t)")
+            )
+            nc.sync.dma_start(out_words[:, cols], y_codes[:, cols].bitcast(I32))
+        for q in range(4):
+            queue = nc.scalar if q % 2 else nc.sync
+            queue.dma_start(out_2[0][4 * q : 4 * q + 4, :].bitcast(I32), y_plane[32 * q : 32 * q + 4, :].bitcast(I32))

@@ -85,6 +85,8 @@ def tile_picked_pqjratiostdgmaxd_none_po_kernel(
         nc.vector.memset(quarter[:], 0.25)
         half_bias = tile("half_bias", [P, 1], F32)
         nc.vector.memset(half_bias[:], 0.5)
+        warm = tile("warm", [P, 1], F32)
+        nc.scalar.activation(warm[:], quarter[:], ACT.Abs_reciprocal_sqrt)
         rows = [tile(f"rows{t}", [P, 2 * S], F32) for t in range(PACK)]
         for t in range(PACK):
             nc.vector.memset(rows[t][:, S : 2 * S], 0.0)
@@ -153,26 +155,25 @@ def tile_picked_pqjratiostdgmaxd_none_po_kernel(
                 nc.scalar.activation(fetched[h][:, 0, t % 2, :], rows[t][:].indirect(n3_l[:]), ACT.Copy)
                 nc.scalar.activation(fetched[h][:, 1, t % 2, :], rows[t][:].indirect(n4_l[:]), ACT.Copy)
 
-        pa = [tile(f"pa{h}", [P, 2, W], F32) for h in range(2)]
-        pb = [tile(f"pb{h}", [P, 2, W], F32) for h in range(2)]
-        size = [tile(f"size{h}", [P, 2, W], F32) for h in range(2)]
-        den2 = [tile(f"den2_{h}", [P, 2, W], F32) for h in range(2)]
-        inv = [tile(f"inv{h}", [P, 2, W], F32) for h in range(2)]
-        for h in range(2):
-            for t in pairs[h]:
-                a_t = rows[t][:, S : 2 * S]
-                nc.scalar.activation(a_t, a_banks[t][:], ACT.Copy, scale=0.0625)
-                nc.scalar.activation(pb[h][:, t % 2, :], a_t.indirect(n2_l[:]), ACT.Copy)
-                nc.scalar.activation(pa[h][:, t % 2, :], a_t.indirect(n1_l[:]), ACT.Copy)
-            nc.scalar.activation(size[h][:], pb[h][:], ACT.Abs)
-            nc.scalar.activation(den2[h][:], size[h][:], ACT.Square, bias=half_bias[:])
-            nc.scalar.activation(inv[h][:], den2[h][:], ACT.Abs_reciprocal_sqrt)
+        pa = tile("pa", [P, PACK, W], F32)
+        pb = tile("pb", [P, PACK, W], F32)
+        size = tile("size", [P, PACK, W], F32)
+        den2 = tile("den2", [P, PACK, W], F32)
+        inv = tile("inv", [P, PACK, W], F32)
+        for t in range(PACK):
+            a_t = tile(f"a_rows{t}", [P, S], F32)
+            nc.vector.tensor_scalar(a_t[:], a_banks[t][:], 0.0625, None, ALU.mult)
+            nc.scalar.activation(pb[:, t, :], a_t[:].indirect(n2_l[:]), ACT.Copy)
+            nc.scalar.activation(pa[:, t, :], a_t[:].indirect(n1_l[:]), ACT.Copy)
+        nc.scalar.activation(size[:], pb[:], ACT.Abs)
+        nc.scalar.activation(den2[:], size[:], ACT.Square, bias=half_bias[:])
+        nc.scalar.activation(inv[:], den2[:], ACT.Abs_reciprocal_sqrt)
 
         sq = [tile(f"sq{h}", [P, 2, 2, S], F32) for h in range(2)]
         centred = [tile(f"centred{h}", [P, 2, S], F32) for h in range(2)]
         spread = [tile(f"spread{h}", [P, 2, S], F32) for h in range(2)]
         inv2 = [tile(f"inv2_{h}", [P, 2, S], F32) for h in range(2)]
-        terms, ra, rb, dt = {}, {}, {}, {}
+        terms = {}
 
         def b_sums(h, slot):
             terms[h] = tile(f"terms{h}", [P, 3, 2, S], F32, slot)
@@ -189,6 +190,8 @@ def tile_picked_pqjratiostdgmaxd_none_po_kernel(
                     centred[h][:, t % 2, :], terms[h][:, 2, t % 2, :], -5.0 / 11.0, rows[t][:, 0:S], ALU.mult, ALU.add
                 )
             nc.vector.tensor_tensor(sq[h][:], terms[h][:, 0:2], terms[h][:, 0:2], ALU.mult)
+
+        def b_root(h):
             nc.vector.scalar_tensor_tensor(spread[h][:], sq[h][:, 0], 0.390625, sq[h][:, 1], ALU.mult, ALU.add)
             nc.scalar.activation(inv2[h][:], spread[h][:], ACT.Abs_reciprocal_sqrt, bias=quarter[:], scale=0.5)
 
@@ -199,48 +202,35 @@ def tile_picked_pqjratiostdgmaxd_none_po_kernel(
                     ALU.mult, ALU.mult,
                 )
 
-        def larger(h, slot):
-            rb[h] = tile(f"rb{h}", [P, 2, W], F32, slot)
-            nc.vector.tensor_tensor(rb[h][:], pa[h][:], pb[h][:], ALU.max)
-
-        def ratio(h, slot):
-            ra[h] = tile(f"ra{h}", [P, 2, W], F32, slot)
-            nc.vector.tensor_tensor(ra[h][:], pa[h][:], inv[h][:], ALU.mult)
-
-        def scatters(h):
-            for t in pairs[h]:
-                dt[t] = tile(f"dt{t}", [P, S], F32)
-                nc.scalar.activation(dt[t][:].indirect(n2_l[:]), rb[h][:, t % 2, :], ACT.Copy)
-            for t in pairs[h]:
-                nc.scalar.activation(dt[t][:].indirect(n1_l[:]), ra[h][:, t % 2, :], ACT.Copy)
-
         def z_round(t):
             nc.vector.tensor_scalar(z_bf[:, :, t], dt[t][:], gn_t[:, t : t + 1], None, ALU.mult)
 
+        dt = [tile(f"dt{t}", [P, S], F32) for t in range(PACK)]
         b_sums(0, "b_staged")
         b_spread(0)
-        larger(0, "b_staged")
+        b_root(0)
         b_sums(1, "terms1")
-        ratio(0, "fetched1")
-        scatters(0)
+        rb = tile("rb", [P, PACK, W], F32, "fetched1")
+        nc.vector.tensor_tensor(rb[:], pa[:], pb[:], ALU.max)
+        for t in range(PACK):
+            nc.scalar.activation(dt[t][:].indirect(n2_l[:]), rb[:, t, :], ACT.Copy)
         b_spread(1)
-        larger(1, "terms1")
-        ratio(1, "sq0")
-        scatters(1)
+        ra = tile("ra", [P, PACK, W], F32, "terms1")
+        nc.vector.tensor_tensor(ra[:], pa[:], inv[:], ALU.mult)
+        b_root(1)
+        for t in range(PACK):
+            nc.scalar.activation(dt[t][:].indirect(n1_l[:]), ra[:, t, :], ACT.Copy)
 
-        w_dealt = [tile(f"w_dealt{i}", [P, N], U32) for i in range(2)]
-        w_plane = tile("w_plane", [P, N], U8)
+        w_dealt = tile("w_dealt", [P, 2, N], U32, "pa")
+        w_plane = tile("w_plane", [P, N], U8, "inv")
         for i in range(2):
-            deal(nc.vector, w_dealt[i][:], w_raw[:, i, :], 4)
+            deal(nc.vector, w_dealt[:, i, :], w_raw[:, i, :], 4)
         deal(nc.vector, w_plane[:], w_bytes_raw[:], 16)
         gm_s = tile("gm_s", [P, PACK], F32)
         nc.vector.tensor_scalar(gm_s[:], gm_t, 0.6875, None, ALU.mult)
 
         z2_rows = tile("z2_rows", [P, PACK, S], BF16)
-        z_bf = tile("z_bf", [P, S, PACK], BF16, "sq1")
         b_finish(0)
-        z_round(0)
-        z_round(1)
         b_finish(1)
         z2_bf = tile("z2_bf", [P, S, PACK], BF16)
         interleave(nc, z2_bf[:], z2_rows[:])
@@ -249,8 +239,9 @@ def tile_picked_pqjratiostdgmaxd_none_po_kernel(
         nc.vector.quantize_mx(
             out=z_codes[1][:].bitcast(FP8X4), scales=z_plane[1][:], in_=z2_bf[:].rearrange("p j t -> p (j t)")
         )
-        z_round(2)
-        z_round(3)
+        z_bf = tile("z_bf", [P, S, PACK], BF16, "z2_rows")
+        for t in range(PACK):
+            z_round(t)
         nc.vector.quantize_mx(
             out=z_codes[0][:].bitcast(FP8X4), scales=z_plane[0][:], in_=z_bf[:].rearrange("p j t -> p (j t)")
         )
@@ -261,7 +252,7 @@ def tile_picked_pqjratiostdgmaxd_none_po_kernel(
                 cols = slice(P * t, P * (t + 1))
                 nc.tensor.matmul_mx(
                     out=h_banks[t][:],
-                    lhsT=w_dealt[i][:, cols].bitcast(FP8X4),
+                    lhsT=w_dealt[:, i, cols].bitcast(FP8X4),
                     lhsT_scale=w_plane[4 * i : P, cols],
                     rhs=z_codes[i][:].bitcast(FP8X4),
                     rhs_scale=z_plane[i][:],
@@ -279,30 +270,37 @@ def tile_picked_pqjratiostdgmaxd_none_po_kernel(
         for c in range(chunks):
             cols = slice(CHUNK * c, CHUNK * (c + 1))
             entries = n5_l[:, CHUNK * MEMBERS // 16 * c : CHUNK * MEMBERS // 16 * (c + 1)]
-            mb = tile(f"mb{c}", [P, PACK, CHUNK, MEMBERS], F32)
+            mb = [tile(f"mb{c}_{h}", [P, 2, CHUNK, MEMBERS], F32) for h in range(2)]
             mx = tile(f"mx{c}", [P, PACK, CHUNK], F32)
             y = tile(f"y{c}", [P, PACK, CHUNK], F32)
             y_bf = tile(f"y_bf{c}", [P, CHUNK, PACK], BF16)
-            for t in range(PACK):
-                nc.scalar.activation(mb[:, t].rearrange("p j m -> p (j m)"), rows[t][:].indirect(entries), ACT.Copy)
-            if c < chunks - 1:
-                half = tile(f"half{c}", [P, PACK * CHUNK, 2], F32)
-                flat = mb[:].rearrange("p t j m -> p (t j) m")
-                nc.vector.tensor_tensor(half[:], flat[:, :, 0:2], flat[:, :, 2:4], ALU.max)
-                nc.vector.tensor_tensor(mx[:].rearrange("p t j -> p (t j)"), half[:, :, 0], half[:, :, 1], ALU.max)
-                for t in range(PACK):
+            last = c == chunks - 1
+            for h in range(2):
+                both_rows = slice(2 * h, 2 * h + 2)
+                for t in pairs[h]:
+                    members = mb[h][:, t % 2]
+                    nc.scalar.activation(members.rearrange("p j m -> p (j m)"), rows[t][:].indirect(entries), ACT.Copy)
+                    if last:
+                        nc.vector.tensor_reduce(mx[:, t, :], members, AXIS.X, ALU.max)
+                        nc.vector.tensor_tensor(y_bf[:, :, t], rows[t][:, cols], mx[:, t, :], ALU.subtract)
+                if not last:
+                    half = tile(f"half{c}_{h}", [P, 2 * CHUNK, 2], F32)
+                    flat = mb[h][:].rearrange("p t j m -> p (t j) m")
+                    nc.vector.tensor_tensor(half[:], flat[:, :, 0:2], flat[:, :, 2:4], ALU.max)
+                    nc.vector.tensor_tensor(
+                        mx[:, both_rows, :].rearrange("p t j -> p (t j)"), half[:, :, 0], half[:, :, 1], ALU.max
+                    )
+                for t in pairs[h]:
                     nc.vector.tensor_tensor(y[:, t, :], rows[t][:, cols], mx[:, t, :], ALU.subtract)
+                if last:
+                    nc.sync.dma_start(out_rows[:, both_rows, cols], y[:, both_rows, :])
+            if not last:
+                nc.sync.dma_start(out_rows[:, :, cols], y[:])
                 interleave(nc, y_bf[:], y[:])
-            else:
-                for t in range(PACK):
-                    nc.vector.tensor_reduce(mx[:, t, :], mb[:, t], AXIS.X, ALU.max)
-                    nc.vector.tensor_tensor(y_bf[:, :, t], rows[t][:, cols], mx[:, t, :], ALU.subtract)
-                    nc.vector.tensor_tensor(y[:, t, :], rows[t][:, cols], mx[:, t, :], ALU.subtract)
-            nc.sync.dma_start(out_rows[:, :, cols], y[:])
             nc.vector.quantize_mx(
                 out=y_codes[:, cols].bitcast(FP8X4), scales=y_plane[:, cols], in_=y_bf[:].rearrange("p j t -> p (j t)")
             )
             nc.sync.dma_start(out_words[:, cols], y_codes[:, cols].bitcast(I32))
         for q in range(4):
-            queue = nc.scalar if q % 2 else nc.sync
+            queue = nc.scalar if q else nc.sync
             queue.dma_start(out_2[0][4 * q : 4 * q + 4, :].bitcast(I32), y_plane[32 * q : 32 * q + 4, :].bitcast(I32))

@@ -18,7 +18,8 @@ AXIS = mybir.AxisListType
 
 P = 128
 PACK = 4
-CHUNK = 64
+CHUNKS = (128, 64, 64)
+WINDOW = 544
 MEMBERS = 4
 
 
@@ -87,9 +88,9 @@ def tile_picked_pqjratiostdgmaxd_none_po_kernel(
         nc.vector.memset(half_bias[:], 0.5)
         warm = tile("warm", [P, 1], F32)
         nc.scalar.activation(warm[:], quarter[:], ACT.Abs_reciprocal_sqrt)
-        rows = [tile(f"rows{t}", [P, 2 * S], F32) for t in range(PACK)]
+        rows = [tile(f"rows{t}", [P, WINDOW], F32) for t in range(PACK)]
         for t in range(PACK):
-            nc.vector.memset(rows[t][:, S : 2 * S], 0.0)
+            nc.vector.memset(rows[t][:, S:WINDOW], 0.0)
 
         def coded_layer(name, codes_l, tokens_l, plane, queue, slots):
             picked_db = tile(f"{name}_db", [P, H], U8, slots[0])
@@ -215,9 +216,9 @@ def tile_picked_pqjratiostdgmaxd_none_po_kernel(
         for t in range(PACK):
             nc.scalar.activation(dt[t][:].indirect(n2_l[:]), rb[:, t, :], ACT.Copy)
         b_spread(1)
-        ra = tile("ra", [P, PACK, W], F32, "terms1")
-        nc.vector.tensor_tensor(ra[:], pa[:], inv[:], ALU.mult)
         b_root(1)
+        ra = tile("ra", [P, PACK, W], F32, "sq1")
+        nc.vector.tensor_tensor(ra[:], pa[:], inv[:], ALU.mult)
         for t in range(PACK):
             nc.scalar.activation(dt[t][:].indirect(n1_l[:]), ra[:, t, :], ACT.Copy)
 
@@ -266,15 +267,15 @@ def tile_picked_pqjratiostdgmaxd_none_po_kernel(
         out_words = words_of(out_1)
         y_codes = tile("y_codes", [P, S], U32)
         y_plane = tile("y_plane", [P, S], U8)
-        chunks = S // CHUNK
-        for c in range(chunks):
-            cols = slice(CHUNK * c, CHUNK * (c + 1))
-            entries = n5_l[:, CHUNK * MEMBERS // 16 * c : CHUNK * MEMBERS // 16 * (c + 1)]
-            mb = [tile(f"mb{c}_{h}", [P, 2, CHUNK, MEMBERS], F32) for h in range(2)]
-            mx = tile(f"mx{c}", [P, PACK, CHUNK], F32)
-            y = tile(f"y{c}", [P, PACK, CHUNK], F32)
-            y_bf = tile(f"y_bf{c}", [P, CHUNK, PACK], BF16)
-            last = c == chunks - 1
+        for c, width in enumerate(CHUNKS):
+            first = sum(CHUNKS[:c])
+            cols = slice(first, first + width)
+            entries = n5_l[:, first * MEMBERS // 16 : (first + width) * MEMBERS // 16]
+            mb = [tile(f"mb{c}_{h}", [P, 2, width, MEMBERS], F32) for h in range(2)]
+            mx = tile(f"mx{c}", [P, PACK, width], F32)
+            y = tile(f"y{c}", [P, PACK, width], F32)
+            y_bf = tile(f"y_bf{c}", [P, width, PACK], BF16)
+            last = c == len(CHUNKS) - 1
             for h in range(2):
                 both_rows = slice(2 * h, 2 * h + 2)
                 for t in pairs[h]:
@@ -284,7 +285,7 @@ def tile_picked_pqjratiostdgmaxd_none_po_kernel(
                         nc.vector.tensor_reduce(mx[:, t, :], members, AXIS.X, ALU.max)
                         nc.vector.tensor_tensor(y_bf[:, :, t], rows[t][:, cols], mx[:, t, :], ALU.subtract)
                 if not last:
-                    half = tile(f"half{c}_{h}", [P, 2 * CHUNK, 2], F32)
+                    half = tile(f"half{c}_{h}", [P, 2 * width, 2], F32)
                     flat = mb[h][:].rearrange("p t j m -> p (t j) m")
                     nc.vector.tensor_tensor(half[:], flat[:, :, 0:2], flat[:, :, 2:4], ALU.max)
                     nc.vector.tensor_tensor(

from contextlib import ExitStack

import concourse.mybir as mybir

K, T, S, N, G, H, W, U = 512, 1024, 256, 512, 2048, 512, 128, 1024
FLOPS = 2 * 2 * K * H * S + 2 * 2 * H * N * S

F32 = mybir.dt.float32
BF16 = mybir.dt.bfloat16
I32 = mybir.dt.int32
U32 = mybir.dt.uint32
U16 = mybir.dt.uint16
U8 = mybir.dt.uint8
FP8X4 = mybir.dt.float8_e4m3fn_x4
ALU = mybir.AluOpType
ACT = mybir.ActivationFunctionType
AXIS = mybir.AxisListType

P = 128
PACK = 4
CHUNKS = (128, 64, 64)
WINDOW = 544
MEMBERS = 4


def words_of(dram):
    return dram[0].rearrange("p n t -> p (n t)").bitcast(I32)


def deal(engine, out, in_, run):
    engine.tensor_copy(
        out=out.rearrange("p (t c i) -> p c t i", t=PACK, i=run),
        in_=in_.rearrange("p (c i t) -> p c t i", t=PACK, i=run),
    )


def interleave(nc, out, in_):
    nc.vector.tensor_copy(
        out=out.rearrange("p (c i) t -> p c t i", i=4),
        in_=in_.rearrange("p t (c i) -> p c t i", i=4),
    )


def tile_picked_pqjratiostdgmaxd_none_po_kernel(
    tc, x_words, x_scales, d_words, d_scales, gn, gm, w1_words, w1_scales, w2_words, w2_scales,
    offs, k1, two, k2, n1, n2, n3, n4, n5, out_0, out_1, out_2,
):
    nc = tc.nc
    with ExitStack() as ctx:
        held = ctx.enter_context(tc.tile_pool(name="held", bufs=1))
        sb = ctx.enter_context(tc.tile_pool(name="sb", bufs=1))
        psum = ctx.enter_context(tc.psum_pool(name="psum", bufs=1))

        def tile(name, shape, dtype, tag=None):
            return sb.tile(shape, dtype, name=name, tag=tag or name, align_bytes=64)

        def load_list(name, dram):
            offsets = held.tile(list(dram.shape), U16, name=name)
            nc.sync.dma_start(offsets[:], dram)
            return offsets

        d_bytes = tile("d_bytes", [P, G], U8)
        x_bytes = tile("x_bytes", [P, T], U8)
        nc.vector.memset(d_bytes[:].bitcast(I32), 0)
        nc.vector.memset(x_bytes[:].bitcast(I32), 0)
        nc.scalar.dma_start(d_bytes[0:P:8, :].bitcast(I32), d_scales[0].bitcast(I32))
        nc.scalar.dma_start(x_bytes[0:P:8, :].bitcast(I32), x_scales[0].bitcast(I32))
        k2_l = load_list("k2_l", k2)
        two_l = load_list("two_l", two)
        k1_l = load_list("k1_l", k1)
        offs_l = load_list("offs_l", offs)
        n3_l = load_list("n3_l", n3)
        x_table = tile("x_table", [P, T], U32)
        d_table = tile("d_table", [P, G], U32)
        nc.sync.dma_start(d_table[:].bitcast(I32), words_of(d_words))
        nc.sync.dma_start(x_table[:].bitcast(I32), words_of(x_words))
        n4_l = load_list("n4_l", n4)
        n2_l = load_list("n2_l", n2)
        n1_l = load_list("n1_l", n1)
        n5_l = load_list("n5_l", n5)

        planes = [tile(f"plane{i}", [P, H + S], U8) for i in range(2)]
        for plane in planes:
            nc.vector.memset(plane[:].bitcast(I32), 0)
        quarter = tile("quarter", [P, 1], F32)
        nc.vector.memset(quarter[:], 0.25)
        half_bias = tile("half_bias", [P, 1], F32)
        nc.vector.memset(half_bias[:], 0.5)
        warm = tile("warm", [P, 1], F32)
        nc.scalar.activation(warm[:], quarter[:], ACT.Abs_reciprocal_sqrt)
        rows = [tile(f"rows{t}", [P, WINDOW], F32) for t in range(PACK)]
        for t in range(PACK):
            nc.vector.memset(rows[t][:, S:WINDOW], 0.0)

        def coded_layer(name, codes_l, tokens_l, plane, queue, slots):
            picked_db = tile(f"{name}_db", [P, H], U8, slots[0])
            picked_xb = tile(f"{name}_xb", [P, S], U8, slots[1])
            staged = tile(f"{name}_staged", [P, H + S], U8)
            nc.vector.tensor_copy(picked_db[:], d_bytes[:].indirect(codes_l[:]))
            nc.vector.tensor_copy(picked_xb[:], x_bytes[:].indirect(tokens_l[:]))
            deal(nc.vector, staged[:, 0:H], picked_db[:], 16)
            nc.vector.tensor_copy(staged[:, H : H + S].bitcast(I32), picked_xb[:].bitcast(I32))
            for q in range(4):
                queue.dma_start(
                    plane[32 * q : 32 * q + 4, :].bitcast(I32),
                    staged[32 * q : 32 * q + 32 : 8, :].bitcast(I32),
                )
            picked_dw = tile(f"{name}_dw", [P, H], U32, slots[2])
            picked_xw = tile(f"{name}_xw", [P, S], U32, slots[3])
            dealt_dw = tile(f"{name}_dealt", [P, H], U32)
            nc.vector.tensor_copy(picked_dw[:], d_table[:].indirect(codes_l[:]))
            nc.vector.tensor_copy(picked_xw[:], x_table[:].indirect(tokens_l[:]))
            deal(nc.vector, dealt_dw[:], picked_dw[:], 4)
            banks = []
            for t in range(PACK):
                bank = psum.tile([P, S], F32, name=f"{name}_bank{t}", tag=f"{name}_bank{t}")
                cols = slice(P * t, P * (t + 1))
                nc.tensor.matmul_mx(
                    out=bank[:],
                    lhsT=dealt_dw[:, cols].bitcast(FP8X4),
                    lhsT_scale=plane[:, cols],
                    rhs=picked_xw[:].bitcast(FP8X4),
                    rhs_scale=plane[:, H : H + S],
                    start=True,
                    stop=True,
                )
                banks.append(bank)
            return banks

        b_banks = coded_layer("b", k2_l, two_l, planes[0], nc.scalar, ("relay", "b_x", "relay", "b_x"))
        gains = tile("gains", [P, 2, 8], F32, "plane0")
        gn_t = gains[:, 0, 0:PACK]
        gm_t = gains[:, 1, 0:PACK]
        nc.sync.dma_start(gn_t, gn.rearrange("(p t) o -> p (t o)", t=PACK))
        nc.sync.dma_start(gm_t, gm.rearrange("(p t) o -> p (t o)", t=PACK))
        a_banks = coded_layer("a", k1_l, offs_l, planes[1], nc.sync, ("relay", "b_staged", "b_staged", "relay"))

        w_raw = tile("w_raw", [P, 2, N], U32, "a_staged")
        nc.sync.dma_start(w_raw[:, 0, :].bitcast(I32), words_of(w1_words))
        nc.sync.dma_start(w_raw[:, 1, :].bitcast(I32), words_of(w2_words))
        w_bytes_raw = tile("w_bytes_raw", [P, N], U8, "plane1")
        nc.vector.memset(w_bytes_raw[:].bitcast(I32), 0)
        for i, scales in enumerate((w1_scales, w2_scales)):
            for q in range(4):
                nc.sync.dma_start(
                    w_bytes_raw[32 * q + 4 * i : 32 * q + 4 * i + 4, :].bitcast(I32),
                    scales[0][4 * q : 4 * q + 4, :].bitcast(I32),
                )

        pairs = ((0, 1), (2, 3))
        fetched = [tile(f"fetched{h}", [P, 2, 2, S], F32) for h in range(2)]
        for h in range(2):
            for t in pairs[h]:
                nc.scalar.activation(rows[t][:, 0:S], b_banks[t][:], ACT.Copy, scale=0.0625)
            for t in pairs[h]:
                nc.scalar.activation(fetched[h][:, 0, t % 2, :], rows[t][:].indirect(n3_l[:]), ACT.Copy)
                nc.scalar.activation(fetched[h][:, 1, t % 2, :], rows[t][:].indirect(n4_l[:]), ACT.Copy)

        pa = tile("pa", [P, PACK, W], F32)
        pb = tile("pb", [P, PACK, W], F32)
        size = tile("size", [P, PACK, W], F32)
        den2 = tile("den2", [P, PACK, W], F32)
        inv = tile("inv", [P, PACK, W], F32)
        for t in range(PACK):
            a_t = tile(f"a_rows{t}", [P, S], F32)
            nc.vector.tensor_scalar(a_t[:], a_banks[t][:], 0.0625, None, ALU.mult)
            nc.scalar.activation(pb[:, t, :], a_t[:].indirect(n2_l[:]), ACT.Copy)
            nc.scalar.activation(pa[:, t, :], a_t[:].indirect(n1_l[:]), ACT.Copy)
        nc.scalar.activation(size[:], pb[:], ACT.Abs)
        nc.scalar.activation(den2[:], size[:], ACT.Square, bias=half_bias[:])
        nc.scalar.activation(inv[:], den2[:], ACT.Abs_reciprocal_sqrt)

        sq = [tile(f"sq{h}", [P, 2, 2, S], F32) for h in range(2)]
        centred = [tile(f"centred{h}", [P, 2, S], F32) for h in range(2)]
        spread = [tile(f"spread{h}", [P, 2, S], F32) for h in range(2)]
        inv2 = [tile(f"inv2_{h}", [P, 2, S], F32) for h in range(2)]
        terms = {}

        def b_sums(h, slot):
            terms[h] = tile(f"terms{h}", [P, 3, 2, S], F32, slot)
            nc.vector.tensor_tensor(terms[h][:, 2], fetched[h][:, 0], fetched[h][:, 1], ALU.add)
            nc.vector.tensor_tensor(terms[h][:, 1], fetched[h][:, 0], fetched[h][:, 1], ALU.subtract)

        def b_spread(h):
            for t in pairs[h]:
                nc.vector.scalar_tensor_tensor(
                    terms[h][:, 0, t % 2, :], terms[h][:, 2, t % 2, :], -0.6, rows[t][:, 0:S], ALU.mult, ALU.add
                )
            for t in pairs[h]:
                nc.vector.scalar_tensor_tensor(
                    centred[h][:, t % 2, :], terms[h][:, 2, t % 2, :], -5.0 / 11.0, rows[t][:, 0:S], ALU.mult, ALU.add
                )
            nc.vector.tensor_tensor(sq[h][:], terms[h][:, 0:2], terms[h][:, 0:2], ALU.mult)

        def b_root(h):
            nc.vector.scalar_tensor_tensor(spread[h][:], sq[h][:, 0], 0.390625, sq[h][:, 1], ALU.mult, ALU.add)
            nc.scalar.activation(inv2[h][:], spread[h][:], ACT.Abs_reciprocal_sqrt, bias=quarter[:], scale=0.5)

        def b_finish(h):
            for t in pairs[h]:
                nc.vector.scalar_tensor_tensor(
                    z2_rows[:, t, :], centred[h][:, t % 2, :], gm_s[:, t : t + 1], inv2[h][:, t % 2, :],
                    ALU.mult, ALU.mult,
                )

        def z_round(t):
            nc.vector.tensor_scalar(z_bf[:, :, t], dt[t][:], gn_t[:, t : t + 1], None, ALU.mult)

        dt = [tile(f"dt{t}", [P, S], F32) for t in range(PACK)]
        b_sums(0, "b_staged")
        b_spread(0)
        b_root(0)
        b_sums(1, "terms1")
        rb = tile("rb", [P, PACK, W], F32, "fetched1")
        nc.vector.tensor_tensor(rb[:], pa[:], pb[:], ALU.max)
        for t in range(PACK):
            nc.scalar.activation(dt[t][:].indirect(n2_l[:]), rb[:, t, :], ACT.Copy)
        b_spread(1)
        b_root(1)
        ra = tile("ra", [P, PACK, W], F32, "sq1")
        nc.vector.tensor_tensor(ra[:], pa[:], inv[:], ALU.mult)
        for t in range(PACK):
            nc.scalar.activation(dt[t][:].indirect(n1_l[:]), ra[:, t, :], ACT.Copy)

        w_dealt = tile("w_dealt", [P, 2, N], U32, "pa")
        w_plane = tile("w_plane", [P, N], U8, "inv")
        for i in range(2):
            deal(nc.vector, w_dealt[:, i, :], w_raw[:, i, :], 4)
        deal(nc.vector, w_plane[:], w_bytes_raw[:], 16)
        gm_s = tile("gm_s", [P, PACK], F32)
        nc.vector.tensor_scalar(gm_s[:], gm_t, 0.6875, None, ALU.mult)

        z2_rows = tile("z2_rows", [P, PACK, S], BF16)
        b_finish(0)
        b_finish(1)
        z2_bf = tile("z2_bf", [P, S, PACK], BF16)
        interleave(nc, z2_bf[:], z2_rows[:])
        z_codes = [tile(f"z_codes{i}", [P, S], U32) for i in range(2)]
        z_plane = [tile(f"z_plane{i}", [P, S], U8) for i in range(2)]
        nc.vector.quantize_mx(
            out=z_codes[1][:].bitcast(FP8X4), scales=z_plane[1][:], in_=z2_bf[:].rearrange("p j t -> p (j t)")
        )
        z_bf = tile("z_bf", [P, S, PACK], BF16, "z2_rows")
        for t in range(PACK):
            z_round(t)
        nc.vector.quantize_mx(
            out=z_codes[0][:].bitcast(FP8X4), scales=z_plane[0][:], in_=z_bf[:].rearrange("p j t -> p (j t)")
        )

        h_banks = [psum.tile([P, S], F32, name=f"h_bank{t}", tag=f"b_bank{t}") for t in range(PACK)]
        for i in (1, 0):
            for t in range(PACK):
                cols = slice(P * t, P * (t + 1))
                nc.tensor.matmul_mx(
                    out=h_banks[t][:],
                    lhsT=w_dealt[:, i, cols].bitcast(FP8X4),
                    lhsT_scale=w_plane[4 * i : P, cols],
                    rhs=z_codes[i][:].bitcast(FP8X4),
                    rhs_scale=z_plane[i][:],
                    start=(i == 1),
                    stop=(i == 0),
                )
        for t in range(PACK):
            nc.vector.tensor_copy(rows[t][:, 0:S], h_banks[t][:])

        out_rows = out_0.rearrange("(p t) j -> p t j", t=PACK)
        out_words = words_of(out_1)
        y_codes = tile("y_codes", [P, S], U32)
        y_plane = tile("y_plane", [P, S], U8)
        for c, width in enumerate(CHUNKS):
            first = sum(CHUNKS[:c])
            cols = slice(first, first + width)
            entries = n5_l[:, first * MEMBERS // 16 : (first + width) * MEMBERS // 16]
            mb = [tile(f"mb{c}_{h}", [P, 2, width, MEMBERS], F32) for h in range(2)]
            mx = tile(f"mx{c}", [P, PACK, width], F32)
            y = tile(f"y{c}", [P, PACK, width], F32)
            y_bf = tile(f"y_bf{c}", [P, width, PACK], BF16)
            last = c == len(CHUNKS) - 1
            for h in range(2):
                both_rows = slice(2 * h, 2 * h + 2)
                for t in pairs[h]:
                    members = mb[h][:, t % 2]
                    nc.scalar.activation(members.rearrange("p j m -> p (j m)"), rows[t][:].indirect(entries), ACT.Copy)
                    if last:
                        nc.vector.tensor_reduce(mx[:, t, :], members, AXIS.X, ALU.max)
                        nc.vector.tensor_tensor(y_bf[:, :, t], rows[t][:, cols], mx[:, t, :], ALU.subtract)
                if not last:
                    half = tile(f"half{c}_{h}", [P, 2 * width, 2], F32)
                    flat = mb[h][:].rearrange("p t j m -> p (t j) m")
                    nc.vector.tensor_tensor(half[:], flat[:, :, 0:2], flat[:, :, 2:4], ALU.max)
                    nc.vector.tensor_tensor(
                        mx[:, both_rows, :].rearrange("p t j -> p (t j)"), half[:, :, 0], half[:, :, 1], ALU.max
                    )
                for t in pairs[h]:
                    nc.vector.tensor_tensor(y[:, t, :], rows[t][:, cols], mx[:, t, :], ALU.subtract)
                if last:
                    nc.sync.dma_start(out_rows[:, both_rows, cols], y[:, both_rows, :])
            if not last:
                nc.sync.dma_start(out_rows[:, :, cols], y[:])
                interleave(nc, y_bf[:], y[:])
            nc.vector.quantize_mx(
                out=y_codes[:, cols].bitcast(FP8X4), scales=y_plane[:, cols], in_=y_bf[:].rearrange("p j t -> p (j t)")
            )
            nc.sync.dma_start(out_words[:, cols], y_codes[:, cols].bitcast(I32))
        for q in range(4):
            queue = nc.scalar if q else nc.sync
            queue.dma_start(out_2[0][4 * q : 4 * q + 4, :].bitcast(I32), y_plane[32 * q : 32 * q + 4, :].bitcast(I32))
